import numpy as np
import ml_dtypes


def mxq(x, axis, fmt="e4m3"):
    dtype, down = {"e4m3": (ml_dtypes.float8_e4m3fn, 7), "e5m2": (ml_dtypes.float8_e5m2, 14)}[fmt]
    v = np.moveaxis(np.asarray(x, np.float32).astype(ml_dtypes.bfloat16).astype(np.float64), axis, -1)
    blocks = v.reshape(v.shape[:-1] + (-1, 32))
    amax = np.abs(blocks).max(-1, keepdims=True)
    byte = np.maximum(np.where(amax > 0, np.frexp(amax)[1] - 1 + 127, 0) - down, 1)
    scale = np.exp2(byte - 127.0)
    codes = (blocks / scale).astype(np.float32).astype(dtype).astype(np.float64)
    return np.moveaxis((codes * scale).reshape(v.shape), -1, axis)


WIDE = False


def mx_kscale(k):
    if not WIDE:
        return np.ones(k)
    levels = np.array([10, -10, 5, -5, 0])
    if k % 512:
        return np.exp2(np.random.permutation(np.resize(levels, k // 32))).repeat(32)
    a = np.empty((k // 512, 16))
    for p in range(k // 512):
        a[p, :8] = np.random.permutation(np.resize(levels, 8))
        for g in range(8):
            far = levels[np.abs(levels - a[p, g]) >= 10]
            a[p, g + 8] = far[np.random.randint(len(far))]
    return np.exp2(a.ravel()).repeat(32)


BF16 = ml_dtypes.bfloat16


def bf(x):
    return np.asarray(x, np.float32).astype(BF16)


def f64(x):
    return np.asarray(x).astype(np.float64)


E2M1 = np.array([0.0, 0.5, 1.0, 1.5, 2.0, 3.0, 4.0, 6.0, -0.0, -0.5, -1.0, -1.5, -2.0, -3.0, -4.0, -6.0])


def pack_weight(w, fmt):
    k, n = w.shape
    w = f64(bf(w)).reshape(k // 32, 32, n)
    amax = np.abs(w).max(1)
    if fmt == "e4m3":
        byte = np.frexp(amax)[1] - 1 + 127 - 7
    else:
        mant, ex = np.frexp(amax / 6.0)
        byte = np.where(mant > 0.5, ex, ex - 1) + 127
    byte = np.clip(np.where(amax > 0, byte, 1), 1, 254)
    scaled = (w * np.exp2(127.0 - byte)[:, None, :]).reshape(k, n).astype(np.float32)
    by_word = np.ascontiguousarray(scaled.reshape(k // 512, 128, 4, n).transpose(0, 1, 3, 2))
    if fmt == "e4m3":
        words = by_word.astype(ml_dtypes.float8_e4m3fn).view(np.uint8)
    else:
        c = by_word.astype(ml_dtypes.float4_e2m1fn).view(np.uint8) & 0xF
        words = c[..., 0::2] | (c[..., 1::2] << 4)
    return np.ascontiguousarray(words), np.ascontiguousarray(byte.astype(np.uint8).reshape(k // 512, 16, n))


def unpack_weight(words, scales, fmt):
    g, p, n, _ = words.shape
    if fmt == "e4m3":
        vals = np.ascontiguousarray(words).view(ml_dtypes.float8_e4m3fn).astype(np.float64)
    else:
        nib = np.empty((g, p, n, 4), np.uint8)
        nib[..., 0::2] = words & 0xF
        nib[..., 1::2] = words >> 4
        vals = E2M1[nib]
    vals = vals * np.repeat(np.exp2(scales.astype(np.float64) - 127.0), 8, axis=1)[..., None]
    return vals.transpose(0, 1, 3, 2).reshape(g * 512, n)
def pack4(w):
    words, scales = pack_weight(w, "e2m1")
    return words.reshape(words.shape[0], 128, -1), scales


def unpack4(words, scales):
    return unpack_weight(words.reshape(words.shape[0], 128, -1, 2), scales, "e2m1")


def planes(Y):
    n, m = Y.shape
    b = f64(bf(Y)).reshape(n // 32, 32, m)
    amax = np.abs(b).max(1)
    byte = np.clip(np.where(amax > 0, np.frexp(amax)[1] - 1 + 127 - 7, 1), 1, 254)
    codes = (b * np.exp2(127.0 - byte)[:, None, :]).reshape(n, m).astype(np.float32).astype(ml_dtypes.float8_e4m3fn).view(np.uint8)
    words = codes.reshape(n // 512, 128, 4, m).transpose(0, 1, 3, 2)
    return np.ascontiguousarray(words), np.ascontiguousarray(byte.astype(np.uint8).reshape(n // 512, 16, m))


M, K, N = 2048, 1024, 1536

PERIOD = 10000.0
HORIZON = 1000.0
SPREAD = 0.7


def setup_inputs():
    s = mx_kscale(K)
    steps = np.random.uniform(0.0, HORIZON, M)
    half = K // 2
    freqs = np.exp(-np.log(PERIOD) * np.arange(half) / half)
    angles = freqs[:, None] * steps[None, :]
    x = np.concatenate([np.cos(angles), np.sin(angles)], axis=0)
    x_words, x_scales = pack_weight(x * s[:, None], "e4m3")
    size = 1.2 * np.exp(SPREAD * np.random.randn(N))
    w = np.random.randn(K, N) / np.sqrt(K) * size[None, :]
    return {
        "x_words": x_words,
        "x_scales": x_scales,
        "w": bf(w / s[:, None]),
        "bias": bf(0.4 * np.random.randn(N)),
    }


def reference(x_words, x_scales, w, bias):
    x = unpack_weight(x_words, x_scales, "e4m3")
    wq = mxq(f64(w), 0, "e4m3")
    z = (x.T @ wq) + f64(bias)[None, :]
    y = z / (1.0 + np.exp(-z))
    Y = y.T
    words, scales = planes(Y)
    return y, words, scales

@@ -1,0 +1,231 @@
+from contextlib import ExitStack
+
+import concourse.mybir as mybir
+from concourse.masks import make_identity
+
+M, K, N = 2048, 1024, 1536
+FLOPS = 2 * M * K * N
+
+F32 = mybir.dt.float32
+BF16 = mybir.dt.bfloat16
+I32 = mybir.dt.int32
+U32 = mybir.dt.uint32
+U8 = mybir.dt.uint8
+FP8X4 = mybir.dt.float8_e4m3fn_x4
+SILU = mybir.ActivationFunctionType.Silu
+
+P = 128
+PACK = 4
+SPAN = P * PACK
+PASSES = K // SPAN
+GROUPS = N // SPAN
+CHUNK = 512
+CHUNKS = M // CHUNK
+BLOCKS = CHUNK // P
+STEPS = GROUPS * CHUNKS
+QUADS = 4
+
+
+def tile_timestep_embedding_silu_g6_kernel(tc, x_words, x_scales, w, bias, out_0, out_1, out_2):
+    nc = tc.nc
+    with ExitStack() as ctx:
+        keep = ctx.enter_context(tc.tile_pool(name="keep", bufs=1))
+        flow = ctx.enter_context(tc.tile_pool(name="flow", bufs=4))
+        psum = ctx.enter_context(tc.psum_pool(name="psum", bufs=1))
+        ctx.enter_context(tc.manual_schedule())
+
+        x_codes = [keep.tile([P, PASSES, CHUNK], U32, name="x_codes%d" % c, align_bytes=64) for c in range(CHUNKS)]
+        x_plane_first = keep.tile([P, PASSES, CHUNK], U8, name="x_plane_first", align_bytes=64)
+        x_plane_rest = keep.tile([P, PASSES, M - CHUNK], U8, name="x_plane_rest", align_bytes=64)
+        w_raw = {}
+        w_codes = {}
+        w_plane = {}
+        for g in range(GROUPS):
+            for k in range(PASSES):
+                w_raw[g, k] = keep.tile([P, PACK, SPAN], BF16, name="w_raw%d%d" % (g, k), align_bytes=64)
+                w_codes[g, k] = keep.tile([P, SPAN], U32, name="w_codes%d%d" % (g, k), align_bytes=64)
+                w_plane[g, k] = keep.tile([P, SPAN], U8, name="w_plane%d%d" % (g, k), align_bytes=64)
+        y_plane = [keep.tile([P, CHUNK], U8, name="y_plane%d" % g, align_bytes=64) for g in range(GROUPS)]
+        bias_sb = keep.tile([P, GROUPS, PACK], BF16, name="bias_sb")
+        ident = keep.tile([P, P], F32, name="ident")
+
+        x_bytes = x_words.rearrange("k p m t -> p k (m t)")
+        y_bytes = out_1.rearrange("g p m t -> g p (m t)")
+
+        def load_w(g, k):
+            rows = w[k * SPAN:(k + 1) * SPAN, g * SPAN:(g + 1) * SPAN]
+            nc.sync.dma_start(out=w_raw[g, k][:], in_=rows.rearrange("(p j) n -> p j n", j=PACK))
+
+        def load_x(c, passes):
+            cols = slice(c * CHUNK * PACK, (c + 1) * CHUNK * PACK)
+            nc.sync.dma_start(out=x_codes[c][:, passes, :].bitcast(I32), in_=x_bytes[:, passes, cols].bitcast(I32))
+
+        def load_x_plane(plane, tokens):
+            for q in range(QUADS):
+                rows = x_scales[:, 4 * q:4 * q + 4, tokens].rearrange("k r m -> r k m")
+                nc.sync.dma_start(out=plane[32 * q:32 * q + 4, :, :].bitcast(I32), in_=rows.bitcast(I32))
+
+        def x_plane(c, k):
+            if c == 0:
+                return x_plane_first[:, k, :]
+            return x_plane_rest[:, k, (c - 1) * CHUNK:c * CHUNK]
+
+        w_grouped = {}
+
+        def group_w(g, k, ts):
+            if (g, k) not in w_grouped:
+                w_grouped[g, k] = flow.tile([P, PACK, P, PACK], BF16, name="w_grouped", bufs=2, align_bytes=64)
+            src = w_raw[g, k][:].rearrange("p j (m t) -> p t m j", t=PACK)
+            nc.vector.tensor_copy(out=w_grouped[g, k][:, ts, :, :], in_=src[:, ts, :, :])
+
+        def quantize_w(g, k, ts):
+            cols = slice(ts.start * P, ts.stop * P)
+            nc.vector.quantize_mx(
+                out=w_codes[g, k][:, cols].bitcast(FP8X4),
+                scales=w_plane[g, k][:, cols],
+                in_=w_grouped[g, k][:, ts, :, :].rearrange("p t m j -> p (t m j)"),
+            )
+
+        acc = {}
+        y_t = {}
+        y_grouped = {}
+        turned = {}
+        y_rows = {}
+
+        def multiply(s, t, k):
+            g, c = divmod(s, CHUNKS)
+            if k == 0:
+                acc[s, t] = psum.tile([P, CHUNK], F32, name="acc", tag="bank%d" % t)
+            cols = slice(t * P, (t + 1) * P)
+            nc.tensor.matmul_mx(
+                out=acc[s, t][:],
+                lhsT=w_codes[g, k][:, cols].bitcast(FP8X4),
+                lhsT_scale=w_plane[g, k][:, cols],
+                rhs=x_codes[c][:, k, :].bitcast(FP8X4),
+                rhs_scale=x_plane(c, k),
+                start=(k == 0),
+                stop=(k == PASSES - 1),
+            )
+
+        def activate(s, t):
+            g = s // CHUNKS
+            if t == 0:
+                y_t[s] = flow.tile([P, PACK, CHUNK], F32, name="y_t")
+            nc.scalar.activation(out=y_t[s][:, t, :], in_=acc[s, t][:], func=SILU, bias=bias_sb[:, g, t:t + 1])
+
+        def turn(s, blocks, first_bank):
+            for i, b in enumerate(blocks):
+                turned[s, b] = psum.tile([P, PACK, P], F32, name="turned", tag="bank%d" % (first_bank + i))
+            if blocks[0] == 0:
+                y_rows[s] = flow.tile([P, BLOCKS, SPAN], F32, name="y_rows")
+                order = [(b, t) for t in range(PACK) for b in blocks]
+            else:
+                order = [(b, t) for b in blocks for t in range(PACK)]
+            for b, t in order:
+                nc.tensor.transpose(turned[s, b][:, t, :], y_t[s][:, t, b * P:(b + 1) * P], ident[:])
+
+        def empty(s, b, on_scalar):
+            dst = y_rows[s][:, b, :].rearrange("m (p t) -> m p t", t=PACK)
+            src = turned[s, b][:].rearrange("m t p -> m p t")
+            if on_scalar:
+                nc.scalar.copy(out=dst, in_=src)
+            else:
+                nc.vector.tensor_copy(out=dst, in_=src)
+
+        def store_rows(s, b0, b1):
+            g, c = divmod(s, CHUNKS)
+            rows = out_0[c * CHUNK + b0 * P:c * CHUNK + b1 * P, g * SPAN:(g + 1) * SPAN]
+            nc.sync.dma_start(out=rows.rearrange("(b m) n -> m b n", m=P), in_=y_rows[s][:, b0:b1, :])
+
+        def group_y(s):
+            y_grouped[s] = flow.tile([P, CHUNK, PACK], BF16, name="y_grouped", bufs=2, align_bytes=64)
+            nc.vector.tensor_copy(
+                out=y_grouped[s][:].rearrange("p (c i) t -> p c t i", i=4),
+                in_=y_t[s][:].rearrange("p t (c i) -> p c t i", i=4),
+            )
+
+        def quantize_y(s):
+            g, c = divmod(s, CHUNKS)
+            y_codes = flow.tile([P, CHUNK], U32, name="y_codes", align_bytes=64)
+            nc.vector.quantize_mx(
+                out=y_codes[:].bitcast(FP8X4),
+                scales=y_plane[g][4 * c:, :],
+                in_=y_grouped[s][:].rearrange("p m t -> p (m t)"),
+            )
+            cols = slice(c * CHUNK * PACK, (c + 1) * CHUNK * PACK)
+            nc.sync.dma_start(out=y_bytes[g][:, cols].bitcast(I32), in_=y_codes[:].bitcast(I32))
+            if c == CHUNKS - 1:
+                for q in range(QUADS):
+                    rows = out_2[g, 4 * q:4 * q + 4, :].rearrange("r (c m) -> c r m", c=CHUNKS)
+                    nc.sync.dma_start(out=rows.bitcast(I32), in_=y_plane[g][32 * q:32 * q + 16, :].bitcast(I32))
+
+        nc.vector.memset(x_plane_first[:].rearrange("p k m -> p (k m)").bitcast(I32), 0)
+        nc.vector.memset(x_plane_rest[:].rearrange("p k m -> p (k m)").bitcast(I32), 0)
+        nc.scalar.dma_start(out=bias_sb[:], in_=bias.rearrange("(g p t) -> p g t", p=P, t=PACK))
+        make_identity(nc, ident[:])
+        load_w(0, 0)
+        load_x(0, slice(0, 1))
+        load_x_plane(x_plane_first, slice(0, CHUNK))
+        load_w(0, 1)
+        load_x(0, slice(1, 2))
+        both = slice(0, PASSES)
+        load_x(1, both)
+        load_w(1, 0)
+        load_x_plane(x_plane_rest, slice(CHUNK, M))
+        load_w(1, 1)
+        load_x(2, both)
+        load_x(3, both)
+        load_w(2, 0)
+        load_w(2, 1)
+
+        for k in range(PASSES):
+            group_w(0, k, slice(0, 1))
+            for t in range(PACK):
+                if t + 1 < PACK:
+                    group_w(0, k, slice(t + 1, t + 2))
+                quantize_w(0, k, slice(t, t + 1))
+                multiply(0, t, k)
+                if k == PASSES - 1:
+                    activate(0, t)
+        whole = slice(0, PACK)
+        group_w(1, 0, whole)
+        quantize_w(1, 0, whole)
+
+        later_w = [(1, 1), (2, 0), (2, 1)]
+        last = STEPS - 1
+        for s in range(STEPS):
+            groups_w = s in (0, 2, 4)
+            if s > 0:
+                for t in range(PACK):
+                    for k in range(PASSES):
+                        multiply(s, t, k)
+                    activate(s, t)
+                turn(s - 1, (2, 3), 6)
+            turn(s, (0, 1), 4)
+            if s == last:
+                turn(s, (2, 3), 0)
+            if s > 0:
+                empty(s - 1, 2, True)
+                empty(s - 1, 3, True)
+                store_rows(s - 1, 2, 4)
+            group_y(s)
+            if s == last:
+                break
+            empty(s, 0, groups_w)
+            empty(s, 1, s == 0)
+            store_rows(s, 0, 2)
+            quantize_y(s)
+            if groups_w:
+                group_w(*later_w[s // 2], whole)
+            if s in (1, 3, 5):
+                quantize_w(*later_w[s // 2], whole)
+
+        empty(last, 0, True)
+        store_rows(last, 0, 1)
+        empty(last, 1, False)
+        store_rows(last, 1, 2)
+        empty(last, 2, True)
+        store_rows(last, 2, 3)
+        quantize_y(last)
+        empty(last, 3, True)
+        store_rows(last, 3, 4)

@@ -34,9 +34,8 @@ def tile_timestep_embedding_silu_g6_kernel(tc, x_words, x_scales, w, bias, out_0
         psum = ctx.enter_context(tc.psum_pool(name="psum", bufs=1))
         ctx.enter_context(tc.manual_schedule())
 
-        x_codes = [keep.tile([P, PASSES, CHUNK], U32, name="x_codes%d" % c, align_bytes=64) for c in range(CHUNKS)]
-        x_plane_first = keep.tile([P, PASSES, CHUNK], U8, name="x_plane_first", align_bytes=64)
-        x_plane_rest = keep.tile([P, PASSES, M - CHUNK], U8, name="x_plane_rest", align_bytes=64)
+        x_codes = keep.tile([P, PASSES, M], U32, name="x_codes", align_bytes=64)
+        x_plane = [keep.tile([P, CHUNK], U8, name="x_plane%d" % k, align_bytes=64) for k in range(PASSES)]
         w_raw = {}
         w_codes = {}
         w_plane = {}
@@ -56,27 +55,23 @@ def tile_timestep_embedding_silu_g6_kernel(tc, x_words, x_scales, w, bias, out_0
             rows = w[k * SPAN:(k + 1) * SPAN, g * SPAN:(g + 1) * SPAN]
             nc.sync.dma_start(out=w_raw[g, k][:], in_=rows.rearrange("(p j) n -> p j n", j=PACK))
 
-        def load_x(c, passes):
-            cols = slice(c * CHUNK * PACK, (c + 1) * CHUNK * PACK)
-            nc.sync.dma_start(out=x_codes[c][:, passes, :].bitcast(I32), in_=x_bytes[:, passes, cols].bitcast(I32))
+        def load_x(c0, c1, passes):
+            src = x_bytes[:, passes, c0 * CHUNK * PACK:c1 * CHUNK * PACK]
+            nc.sync.dma_start(out=x_codes[:, passes, c0 * CHUNK:c1 * CHUNK].bitcast(I32), in_=src.bitcast(I32))
 
-        def load_x_plane(plane, tokens):
+        def load_x_plane(k):
             for q in range(QUADS):
-                rows = x_scales[:, 4 * q:4 * q + 4, tokens].rearrange("k r m -> r k m")
-                nc.sync.dma_start(out=plane[32 * q:32 * q + 4, :, :].bitcast(I32), in_=rows.bitcast(I32))
-
-        def x_plane(c, k):
-            if c == 0:
-                return x_plane_first[:, k, :]
-            return x_plane_rest[:, k, (c - 1) * CHUNK:c * CHUNK]
+                rows = x_scales[k, 4 * q:4 * q + 4, :].rearrange("r (c m) -> c r m", c=CHUNKS)
+                nc.sync.dma_start(out=x_plane[k][32 * q:32 * q + 16, :].bitcast(I32), in_=rows.bitcast(I32))
 
         w_grouped = {}
 
         def group_w(g, k, ts):
             if (g, k) not in w_grouped:
                 w_grouped[g, k] = flow.tile([P, PACK, P, PACK], BF16, name="w_grouped", bufs=2, align_bytes=64)
-            src = w_raw[g, k][:].rearrange("p j (m t) -> p t m j", t=PACK)
-            nc.vector.tensor_copy(out=w_grouped[g, k][:, ts, :, :], in_=src[:, ts, :, :])
+            src = w_raw[g, k][:].rearrange("p j (m t) -> p m t j", t=PACK)
+            dst = w_grouped[g, k][:].rearrange("p t m j -> p m t j")
+            nc.vector.tensor_copy(out=dst[:, :, ts, :], in_=src[:, :, ts, :])
 
         def quantize_w(g, k, ts):
             cols = slice(ts.start * P, ts.stop * P)
@@ -86,14 +81,17 @@ def tile_timestep_embedding_silu_g6_kernel(tc, x_words, x_scales, w, bias, out_0
                 in_=w_grouped[g, k][:, ts, :, :].rearrange("p t m j -> p (t m j)"),
             )
 
+        order = [(0, c) for c in range(CHUNKS)] + [(g, c) for c in range(CHUNKS) for g in range(1, GROUPS)]
+        y_codes = {}
         acc = {}
         y_t = {}
         y_grouped = {}
         turned = {}
         y_rows = {}
+        y_wide = {}
 
         def multiply(s, t, k):
-            g, c = divmod(s, CHUNKS)
+            g, c = order[s]
             if k == 0:
                 acc[s, t] = psum.tile([P, CHUNK], F32, name="acc", tag="bank%d" % t)
             cols = slice(t * P, (t + 1) * P)
@@ -101,14 +99,14 @@ def tile_timestep_embedding_silu_g6_kernel(tc, x_words, x_scales, w, bias, out_0
                 out=acc[s, t][:],
                 lhsT=w_codes[g, k][:, cols].bitcast(FP8X4),
                 lhsT_scale=w_plane[g, k][:, cols],
-                rhs=x_codes[c][:, k, :].bitcast(FP8X4),
-                rhs_scale=x_plane(c, k),
+                rhs=x_codes[:, k, c * CHUNK:(c + 1) * CHUNK].bitcast(FP8X4),
+                rhs_scale=x_plane[k][4 * c:, :],
                 start=(k == 0),
                 stop=(k == PASSES - 1),
             )
 
         def activate(s, t):
-            g = s // CHUNKS
+            g = order[s][0]
             if t == 0:
                 y_t[s] = flow.tile([P, PACK, CHUNK], F32, name="y_t")
             nc.scalar.activation(out=y_t[s][:, t, :], in_=acc[s, t][:], func=SILU, bias=bias_sb[:, g, t:t + 1])
@@ -117,11 +115,17 @@ def tile_timestep_embedding_silu_g6_kernel(tc, x_words, x_scales, w, bias, out_0
             for i, b in enumerate(blocks):
                 turned[s, b] = psum.tile([P, PACK, P], F32, name="turned", tag="bank%d" % (first_bank + i))
             if blocks[0] == 0:
-                y_rows[s] = flow.tile([P, BLOCKS, SPAN], F32, name="y_rows")
-                order = [(b, t) for t in range(PACK) for b in blocks]
+                g, c = order[s]
+                if g == 0:
+                    y_rows[s] = flow.tile([P, BLOCKS, SPAN], F32, name="y_rows_first")
+                elif g == 1:
+                    y_wide[c] = flow.tile([P, BLOCKS, 2 * SPAN], F32, name="y_wide", bufs=3)
+                if g > 0:
+                    y_rows[s] = y_wide[c][:, :, (g - 1) * SPAN:g * SPAN]
+                pairs = [(b, t) for t in range(PACK) for b in blocks]
             else:
-                order = [(b, t) for b in blocks for t in range(PACK)]
-            for b, t in order:
+                pairs = [(b, t) for b in blocks for t in range(PACK)]
+            for b, t in pairs:
                 nc.tensor.transpose(turned[s, b][:, t, :], y_t[s][:, t, b * P:(b + 1) * P], ident[:])
 
         def empty(s, b, on_scalar):
@@ -133,9 +137,14 @@ def tile_timestep_embedding_silu_g6_kernel(tc, x_words, x_scales, w, bias, out_0
                 nc.vector.tensor_copy(out=dst, in_=src)
 
         def store_rows(s, b0, b1):
-            g, c = divmod(s, CHUNKS)
-            rows = out_0[c * CHUNK + b0 * P:c * CHUNK + b1 * P, g * SPAN:(g + 1) * SPAN]
-            nc.sync.dma_start(out=rows.rearrange("(b m) n -> m b n", m=P), in_=y_rows[s][:, b0:b1, :])
+            g, c = order[s]
+            tokens = slice(c * CHUNK + b0 * P, c * CHUNK + b1 * P)
+            if g == 0 or c == CHUNKS - 1:
+                rows = out_0[tokens, g * SPAN:(g + 1) * SPAN]
+                nc.sync.dma_start(out=rows.rearrange("(b m) n -> m b n", m=P), in_=y_rows[s][:, b0:b1, :])
+            elif g == GROUPS - 1:
+                rows = out_0[tokens, SPAN:]
+                nc.sync.dma_start(out=rows.rearrange("(b m) n -> m b n", m=P), in_=y_wide[c][:, b0:b1, :])
 
         def group_y(s):
             y_grouped[s] = flow.tile([P, CHUNK, PACK], BF16, name="y_grouped", bufs=2, align_bytes=64)
@@ -145,56 +154,66 @@ def tile_timestep_embedding_silu_g6_kernel(tc, x_words, x_scales, w, bias, out_0
             )
 
         def quantize_y(s):
-            g, c = divmod(s, CHUNKS)
-            y_codes = flow.tile([P, CHUNK], U32, name="y_codes", align_bytes=64)
+            g, c = order[s]
+            if c % 2 == 0:
+                y_codes[g] = flow.tile([P, 2 * CHUNK], U32, name="y_codes", align_bytes=64)
+            half = slice(c % 2 * CHUNK, (c % 2 + 1) * CHUNK)
             nc.vector.quantize_mx(
-                out=y_codes[:].bitcast(FP8X4),
+                out=y_codes[g][:, half].bitcast(FP8X4),
                 scales=y_plane[g][4 * c:, :],
                 in_=y_grouped[s][:].rearrange("p m t -> p (m t)"),
             )
-            cols = slice(c * CHUNK * PACK, (c + 1) * CHUNK * PACK)
-            nc.sync.dma_start(out=y_bytes[g][:, cols].bitcast(I32), in_=y_codes[:].bitcast(I32))
+            if g > 0 and c >= 2:
+                cols = slice(c * CHUNK * PACK, (c + 1) * CHUNK * PACK)
+                nc.sync.dma_start(out=y_bytes[g][:, cols].bitcast(I32), in_=y_codes[g][:, half].bitcast(I32))
+            elif c % 2 == 1:
+                cols = slice((c - 1) * CHUNK * PACK, (c + 1) * CHUNK * PACK)
+                nc.sync.dma_start(out=y_bytes[g][:, cols].bitcast(I32), in_=y_codes[g][:].bitcast(I32))
             if c == CHUNKS - 1:
                 for q in range(QUADS):
                     rows = out_2[g, 4 * q:4 * q + 4, :].rearrange("r (c m) -> c r m", c=CHUNKS)
                     nc.sync.dma_start(out=rows.bitcast(I32), in_=y_plane[g][32 * q:32 * q + 16, :].bitcast(I32))
 
-        nc.vector.memset(x_plane_first[:].rearrange("p k m -> p (k m)").bitcast(I32), 0)
-        nc.vector.memset(x_plane_rest[:].rearrange("p k m -> p (k m)").bitcast(I32), 0)
+        for k in range(PASSES):
+            nc.vector.memset(x_plane[k][:].bitcast(I32), 0)
         nc.scalar.dma_start(out=bias_sb[:], in_=bias.rearrange("(g p t) -> p g t", p=P, t=PACK))
         make_identity(nc, ident[:])
-        load_w(0, 0)
-        load_x(0, slice(0, 1))
-        load_x_plane(x_plane_first, slice(0, CHUNK))
-        load_w(0, 1)
-        load_x(0, slice(1, 2))
+        for k in range(PASSES):
+            load_w(0, k)
+            load_x(0, 1, slice(k, k + 1))
+            load_x_plane(k)
         both = slice(0, PASSES)
-        load_x(1, both)
         load_w(1, 0)
-        load_x_plane(x_plane_rest, slice(CHUNK, M))
+        load_x(1, 2, both)
         load_w(1, 1)
-        load_x(2, both)
-        load_x(3, both)
+        load_x(2, 4, both)
         load_w(2, 0)
         load_w(2, 1)
 
+        halves = (slice(0, 2), slice(2, 4))
         for k in range(PASSES):
-            group_w(0, k, slice(0, 1))
-            for t in range(PACK):
-                if t + 1 < PACK:
-                    group_w(0, k, slice(t + 1, t + 2))
-                quantize_w(0, k, slice(t, t + 1))
-                multiply(0, t, k)
-                if k == PASSES - 1:
-                    activate(0, t)
-        whole = slice(0, PACK)
-        group_w(1, 0, whole)
-        quantize_w(1, 0, whole)
+            for ts in halves:
+                group_w(0, k, ts)
+            for ts in halves:
+                quantize_w(0, k, ts)
+                for t in range(ts.start, ts.stop):
+                    multiply(0, t, k)
+                    if k == PASSES - 1:
+                        activate(0, t)
+        for ts in halves:
+            group_w(1, 0, ts)
+        for ts in halves:
+            quantize_w(1, 0, ts)
 
-        later_w = [(1, 1), (2, 0), (2, 1)]
+        later_w = [
+            [(1, 1, halves[0]), (1, 1, halves[1])],
+            [(2, 0, halves[0]), (2, 0, halves[1])],
+            [(2, 1, halves[0])],
+            [(2, 1, halves[1])],
+        ]
         last = STEPS - 1
         for s in range(STEPS):
-            groups_w = s in (0, 2, 4)
+            w_work = later_w[s] if s < len(later_w) else []
             if s > 0:
                 for t in range(PACK):
                     for k in range(PASSES):
@@ -211,14 +230,14 @@ def tile_timestep_embedding_silu_g6_kernel(tc, x_words, x_scales, w, bias, out_0
             group_y(s)
             if s == last:
                 break
-            empty(s, 0, groups_w)
+            empty(s, 0, s <= 2)
             empty(s, 1, s == 0)
             store_rows(s, 0, 2)
+            for piece in w_work:
+                group_w(*piece)
             quantize_y(s)
-            if groups_w:
-                group_w(*later_w[s // 2], whole)
-            if s in (1, 3, 5):
-                quantize_w(*later_w[s // 2], whole)
+            for piece in w_work:
+                quantize_w(*piece)
 
         empty(last, 0, True)
         store_rows(last, 0, 1)

@@ -24,6 +24,7 @@ CHUNKS = M // CHUNK
 BLOCKS = CHUNK // P
 STEPS = GROUPS * CHUNKS
 QUADS = 4
+BANKS = 8
 
 
 def tile_timestep_embedding_silu_g6_kernel(tc, x_words, x_scales, w, bias, out_0, out_1, out_2):
@@ -81,52 +82,54 @@ def tile_timestep_embedding_silu_g6_kernel(tc, x_words, x_scales, w, bias, out_0
                 in_=w_grouped[g, k][:, ts, :, :].rearrange("p t m j -> p (t m j)"),
             )
 
-        order = [(0, c) for c in range(CHUNKS)] + [(g, c) for c in range(CHUNKS) for g in range(1, GROUPS)]
         y_codes = {}
         acc = {}
         y_t = {}
         y_grouped = {}
         turned = {}
         y_rows = {}
-        y_wide = {}
+        fills_so_far = list(reversed(range(200)))
 
-        def multiply(s, t, k):
-            g, c = order[s]
+        def next_bank(shape):
+            return psum.tile(shape, F32, name="bank", tag="bank%d" % (fills_so_far.pop() % BANKS))
+
+        def multiply(s, t, k, b0=0, b1=BLOCKS):
+            g, c = divmod(s, CHUNKS)
             if k == 0:
-                acc[s, t] = psum.tile([P, CHUNK], F32, name="acc", tag="bank%d" % t)
+                acc[s, t, b0] = next_bank([P, (b1 - b0) * P])
             cols = slice(t * P, (t + 1) * P)
             nc.tensor.matmul_mx(
-                out=acc[s, t][:],
+                out=acc[s, t, b0][:],
                 lhsT=w_codes[g, k][:, cols].bitcast(FP8X4),
                 lhsT_scale=w_plane[g, k][:, cols],
-                rhs=x_codes[:, k, c * CHUNK:(c + 1) * CHUNK].bitcast(FP8X4),
-                rhs_scale=x_plane[k][4 * c:, :],
+                rhs=x_codes[:, k, c * CHUNK + b0 * P:c * CHUNK + b1 * P].bitcast(FP8X4),
+                rhs_scale=x_plane[k][4 * c:, b0 * P:b1 * P],
                 start=(k == 0),
                 stop=(k == PASSES - 1),
             )
 
-        def activate(s, t):
-            g = order[s][0]
-            if t == 0:
+        def activate(s, t, b0=0, b1=BLOCKS):
+            g = s // CHUNKS
+            if s not in y_t:
                 y_t[s] = flow.tile([P, PACK, CHUNK], F32, name="y_t")
-            nc.scalar.activation(out=y_t[s][:, t, :], in_=acc[s, t][:], func=SILU, bias=bias_sb[:, g, t:t + 1])
+            nc.scalar.activation(
+                out=y_t[s][:, t, b0 * P:b1 * P], in_=acc[s, t, b0][:], func=SILU, bias=bias_sb[:, g, t:t + 1]
+            )
 
-        def turn(s, blocks, first_bank):
-            for i, b in enumerate(blocks):
-                turned[s, b] = psum.tile([P, PACK, P], F32, name="turned", tag="bank%d" % (first_bank + i))
-            if blocks[0] == 0:
-                g, c = order[s]
-                if g == 0:
-                    y_rows[s] = flow.tile([P, BLOCKS, SPAN], F32, name="y_rows_first")
-                elif g == 1:
-                    y_wide[c] = flow.tile([P, BLOCKS, 2 * SPAN], F32, name="y_wide", bufs=3)
-                if g > 0:
-                    y_rows[s] = y_wide[c][:, :, (g - 1) * SPAN:g * SPAN]
-                pairs = [(b, t) for t in range(PACK) for b in blocks]
-            else:
-                pairs = [(b, t) for b in blocks for t in range(PACK)]
-            for b, t in pairs:
-                nc.tensor.transpose(turned[s, b][:, t, :], y_t[s][:, t, b * P:(b + 1) * P], ident[:])
+        def embed(s, b0=0, b1=BLOCKS):
+            for t in range(PACK):
+                for k in range(PASSES):
+                    multiply(s, t, k, b0, b1)
+                activate(s, t, b0, b1)
+
+        def turn(s, b0, b1):
+            if s not in y_rows:
+                y_rows[s] = flow.tile([P, BLOCKS, SPAN], F32, name="y_rows", bufs=5)
+            for b in range(b0, b1):
+                turned[s, b] = next_bank([P, PACK, P])
+            for t in range(PACK):
+                for b in range(b0, b1):
+                    nc.tensor.transpose(turned[s, b][:, t, :], y_t[s][:, t, b * P:(b + 1) * P], ident[:])
 
         def empty(s, b, on_scalar):
             dst = y_rows[s][:, b, :].rearrange("m (p t) -> m p t", t=PACK)
@@ -137,39 +140,30 @@ def tile_timestep_embedding_silu_g6_kernel(tc, x_words, x_scales, w, bias, out_0
                 nc.vector.tensor_copy(out=dst, in_=src)
 
         def store_rows(s, b0, b1):
-            g, c = order[s]
-            tokens = slice(c * CHUNK + b0 * P, c * CHUNK + b1 * P)
-            if g == 0 or c == CHUNKS - 1:
-                rows = out_0[tokens, g * SPAN:(g + 1) * SPAN]
-                nc.sync.dma_start(out=rows.rearrange("(b m) n -> m b n", m=P), in_=y_rows[s][:, b0:b1, :])
-            elif g == GROUPS - 1:
-                rows = out_0[tokens, SPAN:]
-                nc.sync.dma_start(out=rows.rearrange("(b m) n -> m b n", m=P), in_=y_wide[c][:, b0:b1, :])
+            g, c = divmod(s, CHUNKS)
+            rows = out_0[c * CHUNK + b0 * P:c * CHUNK + b1 * P, g * SPAN:(g + 1) * SPAN]
+            nc.sync.dma_start(out=rows.rearrange("(b m) n -> m b n", m=P), in_=y_rows[s][:, b0:b1, :])
 
-        def group_y(s):
-            y_grouped[s] = flow.tile([P, CHUNK, PACK], BF16, name="y_grouped", bufs=2, align_bytes=64)
+        def group_y(s, b0=0, b1=BLOCKS):
+            y_grouped[s, b0] = flow.tile([P, (b1 - b0) * P, PACK], BF16, name="y_grouped", bufs=3, align_bytes=64)
             nc.vector.tensor_copy(
-                out=y_grouped[s][:].rearrange("p (c i) t -> p c t i", i=4),
-                in_=y_t[s][:].rearrange("p t (c i) -> p c t i", i=4),
+                out=y_grouped[s, b0][:].rearrange("p (c i) t -> p c t i", i=4),
+                in_=y_t[s][:, :, b0 * P:b1 * P].rearrange("p t (c i) -> p c t i", i=4),
             )
 
-        def quantize_y(s):
-            g, c = order[s]
-            if c % 2 == 0:
-                y_codes[g] = flow.tile([P, 2 * CHUNK], U32, name="y_codes", align_bytes=64)
-            half = slice(c % 2 * CHUNK, (c % 2 + 1) * CHUNK)
+        def quantize_y(s, b0=0, b1=BLOCKS):
+            g, c = divmod(s, CHUNKS)
+            if g not in y_codes:
+                y_codes[g] = flow.tile([P, M], U32, name="y_codes", bufs=2, align_bytes=64)
             nc.vector.quantize_mx(
-                out=y_codes[g][:, half].bitcast(FP8X4),
-                scales=y_plane[g][4 * c:, :],
-                in_=y_grouped[s][:].rearrange("p m t -> p (m t)"),
+                out=y_codes[g][:, c * CHUNK + b0 * P:c * CHUNK + b1 * P].bitcast(FP8X4),
+                scales=y_plane[g][4 * c:, b0 * P:b1 * P],
+                in_=y_grouped[s, b0][:].rearrange("p m t -> p (m t)"),
             )
-            if g > 0 and c >= 2:
-                cols = slice(c * CHUNK * PACK, (c + 1) * CHUNK * PACK)
-                nc.sync.dma_start(out=y_bytes[g][:, cols].bitcast(I32), in_=y_codes[g][:, half].bitcast(I32))
-            elif c % 2 == 1:
-                cols = slice((c - 1) * CHUNK * PACK, (c + 1) * CHUNK * PACK)
-                nc.sync.dma_start(out=y_bytes[g][:, cols].bitcast(I32), in_=y_codes[g][:].bitcast(I32))
-            if c == CHUNKS - 1:
+
+        def store_codes(g, m0, m1):
+            nc.sync.dma_start(out=y_bytes[g][:, m0 * PACK:m1 * PACK].bitcast(I32), in_=y_codes[g][:, m0:m1].bitcast(I32))
+            if m1 == M:
                 for q in range(QUADS):
                     rows = out_2[g, 4 * q:4 * q + 4, :].rearrange("r (c m) -> c r m", c=CHUNKS)
                     nc.sync.dma_start(out=rows.bitcast(I32), in_=y_plane[g][32 * q:32 * q + 16, :].bitcast(I32))
@@ -183,10 +177,10 @@ def tile_timestep_embedding_silu_g6_kernel(tc, x_words, x_scales, w, bias, out_0
             load_x(0, 1, slice(k, k + 1))
             load_x_plane(k)
         both = slice(0, PASSES)
-        load_w(1, 0)
         load_x(1, 2, both)
-        load_w(1, 1)
+        load_w(1, 0)
         load_x(2, 4, both)
+        load_w(1, 1)
         load_w(2, 0)
         load_w(2, 1)
 
@@ -200,51 +194,87 @@ def tile_timestep_embedding_silu_g6_kernel(tc, x_words, x_scales, w, bias, out_0
                     multiply(0, t, k)
                     if k == PASSES - 1:
                         activate(0, t)
-        for ts in halves:
-            group_w(1, 0, ts)
-        for ts in halves:
-            quantize_w(1, 0, ts)
 
-        later_w = [
-            [(1, 1, halves[0]), (1, 1, halves[1])],
-            [(2, 0, halves[0]), (2, 0, halves[1])],
-            [(2, 1, halves[0])],
-            [(2, 1, halves[1])],
-        ]
-        last = STEPS - 1
-        for s in range(STEPS):
-            w_work = later_w[s] if s < len(later_w) else []
+        later_w = [(g, k) for g in range(1, GROUPS) for k in range(PASSES)]
+        for s in range(0, 2 * len(later_w), 2):
+            g, c = divmod(s, CHUNKS)
             if s > 0:
-                for t in range(PACK):
-                    for k in range(PASSES):
-                        multiply(s, t, k)
-                    activate(s, t)
-                turn(s - 1, (2, 3), 6)
-            turn(s, (0, 1), 4)
-            if s == last:
-                turn(s, (2, 3), 0)
+                embed(s)
+            embed(s + 1)
+            for ts in halves:
+                group_w(*later_w[s // 2], ts)
+            group_y(s)
+            quantize_w(*later_w[s // 2], slice(0, PACK))
+            quantize_y(s)
+            group_y(s + 1)
+            if s > 0:
+                turn(s - 1, 2, 4)
+            turn(s, 0, 2)
+            turn(s, 2, 4)
+            turn(s + 1, 0, 2)
             if s > 0:
                 empty(s - 1, 2, True)
                 empty(s - 1, 3, True)
                 store_rows(s - 1, 2, 4)
-            group_y(s)
-            if s == last:
-                break
-            empty(s, 0, s <= 2)
-            empty(s, 1, s == 0)
-            store_rows(s, 0, 2)
-            for piece in w_work:
-                group_w(*piece)
-            quantize_y(s)
-            for piece in w_work:
-                quantize_w(*piece)
+            for b in range(BLOCKS):
+                empty(s, b, b < 2 or s == 0)
+            store_rows(s, 0, 4)
+            empty(s + 1, 0, False)
+            empty(s + 1, 1, False)
+            store_rows(s + 1, 0, 2)
+            quantize_y(s + 1)
+            store_codes(g, c * CHUNK, (c + 2) * CHUNK)
 
-        empty(last, 0, True)
-        store_rows(last, 0, 1)
-        empty(last, 1, False)
-        store_rows(last, 1, 2)
-        empty(last, 2, True)
-        store_rows(last, 2, 3)
-        quantize_y(last)
-        empty(last, 3, True)
-        store_rows(last, 3, 4)
+        g = GROUPS - 1
+        for s in (8, 9):
+            c = s % CHUNKS
+            embed(s)
+            group_y(s)
+            turn(s - 1, 2, 4)
+            turn(s, 0, 2)
+            empty(s - 1, 2, True)
+            empty(s - 1, 3, True)
+            store_rows(s - 1, 2, 4)
+            empty(s, 0, False)
+            empty(s, 1, False)
+            store_rows(s, 0, 2)
+            quantize_y(s)
+            store_codes(g, c * CHUNK, (c + 1) * CHUNK)
+
+        s = 10
+        embed(s)
+        group_y(s)
+        turn(s - 1, 2, 4)
+        turn(s, 0, 2)
+        turn(s, 2, 4)
+        empty(s - 1, 2, True)
+        empty(s - 1, 3, True)
+        store_rows(s - 1, 2, 4)
+        empty(s, 0, False)
+        empty(s, 1, True)
+        store_rows(s, 0, 2)
+        empty(s, 2, False)
+        empty(s, 3, False)
+        store_rows(s, 2, 4)
+        quantize_y(s)
+        store_codes(g, 2 * CHUNK, 3 * CHUNK)
+
+        s = 11
+        embed(s, 0, 2)
+        embed(s, 2, 4)
+        turn(s, 0, 2)
+        turn(s, 2, 4)
+        group_y(s, 0, 2)
+        quantize_y(s, 0, 2)
+        store_codes(g, 3 * CHUNK, 3 * CHUNK + 2 * P)
+        empty(s, 0, False)
+        store_rows(s, 0, 1)
+        group_y(s, 2, 4)
+        empty(s, 1, True)
+        store_rows(s, 1, 2)
+        empty(s, 2, True)
+        store_rows(s, 2, 3)
+        quantize_y(s, 2, 4)
+        empty(s, 3, True)
+        store_rows(s, 3, 4)
+        store_codes(g, 3 * CHUNK + 2 * P, M)

@@ -25,6 +25,9 @@ BLOCKS = CHUNK // P
 STEPS = GROUPS * CHUNKS
 QUADS = 4
 BANKS = 8
+PLAN = [('double', 'W g0 Q q0 S0 S1 V2 V3 g1 S4 V5 q1'), ('double', 'W g0 Q S0 S1 S2 S3 V4 V5 g1 V6 S7 q0 q1'), ('double', 'W g0 Q S0 S1 S2 S3 V4 V5 g1 V6 S7 q0 q1'), ('single', 'S0 S1 V2 W S3 g0 Q q0'), ('single', 'S0 S1 V2 V3 g0 q0'), ('single', 'S0 S1 V2 V3 g0 q0'), ('single', 'S0 S1 V2 V3 g0 q0'), ('whole', 'V0 S1 S2 S3 g0 V4 V5 q0'), ('last', 'g0 S0 S1 g1 V2 q0 S3 q1')]
+SINGLY = (0, 1)
+ONCE = True
 
 
 def tile_timestep_embedding_silu_g6_kernel(tc, x_words, x_scales, w, bias, out_0, out_1, out_2):
@@ -111,7 +114,7 @@ def tile_timestep_embedding_silu_g6_kernel(tc, x_words, x_scales, w, bias, out_0
         def activate(s, t, b0=0, b1=BLOCKS):
             g = s // CHUNKS
             if s not in y_t:
-                y_t[s] = flow.tile([P, PACK, CHUNK], F32, name="y_t")
+                y_t[s] = flow.tile([P, PACK, CHUNK], F32, name="y_t", bufs=5)
             nc.scalar.activation(
                 out=y_t[s][:, t, b0 * P:b1 * P], in_=acc[s, t, b0][:], func=SILU, bias=bias_sb[:, g, t:t + 1]
             )
@@ -124,7 +127,7 @@ def tile_timestep_embedding_silu_g6_kernel(tc, x_words, x_scales, w, bias, out_0
 
         def turn(s, b0, b1):
             if s not in y_rows:
-                y_rows[s] = flow.tile([P, BLOCKS, SPAN], F32, name="y_rows", bufs=5)
+                y_rows[s] = flow.tile([P, BLOCKS, SPAN], F32, name="y_rows", bufs=6)
             for b in range(b0, b1):
                 turned[s, b] = next_bank([P, PACK, P])
             for t in range(PACK):
@@ -188,7 +191,6 @@ def tile_timestep_embedding_silu_g6_kernel(tc, x_words, x_scales, w, bias, out_0
         for k in range(PASSES):
             for ts in halves:
                 group_w(0, k, ts)
-            for ts in halves:
                 quantize_w(0, k, ts)
                 for t in range(ts.start, ts.stop):
                     multiply(0, t, k)
@@ -196,85 +198,49 @@ def tile_timestep_embedding_silu_g6_kernel(tc, x_words, x_scales, w, bias, out_0
                         activate(0, t)
 
         later_w = [(g, k) for g in range(1, GROUPS) for k in range(PASSES)]
-        for s in range(0, 2 * len(later_w), 2):
-            g, c = divmod(s, CHUNKS)
-            if s > 0:
-                embed(s)
-            embed(s + 1)
-            for ts in halves:
-                group_w(*later_w[s // 2], ts)
-            group_y(s)
-            quantize_w(*later_w[s // 2], slice(0, PACK))
-            quantize_y(s)
-            group_y(s + 1)
-            if s > 0:
-                turn(s - 1, 2, 4)
-            turn(s, 0, 2)
-            turn(s, 2, 4)
-            turn(s + 1, 0, 2)
-            if s > 0:
-                empty(s - 1, 2, True)
-                empty(s - 1, 3, True)
-                store_rows(s - 1, 2, 4)
-            for b in range(BLOCKS):
-                empty(s, b, b < 2 or s == 0)
-            store_rows(s, 0, 4)
-            empty(s + 1, 0, False)
-            empty(s + 1, 1, False)
-            store_rows(s + 1, 0, 2)
-            quantize_y(s + 1)
-            store_codes(g, c * CHUNK, (c + 2) * CHUNK)
-
-        g = GROUPS - 1
-        for s in (8, 9):
-            c = s % CHUNKS
-            embed(s)
-            group_y(s)
-            turn(s - 1, 2, 4)
-            turn(s, 0, 2)
-            empty(s - 1, 2, True)
-            empty(s - 1, 3, True)
-            store_rows(s - 1, 2, 4)
-            empty(s, 0, False)
-            empty(s, 1, False)
-            store_rows(s, 0, 2)
-            quantize_y(s)
-            store_codes(g, c * CHUNK, (c + 1) * CHUNK)
-
-        s = 10
-        embed(s)
-        group_y(s)
-        turn(s - 1, 2, 4)
-        turn(s, 0, 2)
-        turn(s, 2, 4)
-        empty(s - 1, 2, True)
-        empty(s - 1, 3, True)
-        store_rows(s - 1, 2, 4)
-        empty(s, 0, False)
-        empty(s, 1, True)
-        store_rows(s, 0, 2)
-        empty(s, 2, False)
-        empty(s, 3, False)
-        store_rows(s, 2, 4)
-        quantize_y(s)
-        store_codes(g, 2 * CHUNK, 3 * CHUNK)
-
-        s = 11
-        embed(s, 0, 2)
-        embed(s, 2, 4)
-        turn(s, 0, 2)
-        turn(s, 2, 4)
-        group_y(s, 0, 2)
-        quantize_y(s, 0, 2)
-        store_codes(g, 3 * CHUNK, 3 * CHUNK + 2 * P)
-        empty(s, 0, False)
-        store_rows(s, 0, 1)
-        group_y(s, 2, 4)
-        empty(s, 1, True)
-        store_rows(s, 1, 2)
-        empty(s, 2, True)
-        store_rows(s, 2, 3)
-        quantize_y(s, 2, 4)
-        empty(s, 3, True)
-        store_rows(s, 3, 4)
-        store_codes(g, 3 * CHUNK + 2 * P, M)
+        emptied = set()
+        s = 0
+        waiting = []
+        for i, (kind, order) in enumerate(PLAN):
+            steps = [s, s + 1] if kind == "double" else [s]
+            for u in steps:
+                if kind == "last":
+                    embed(u, 0, 2)
+                    embed(u, 2, 4)
+                elif u > 0:
+                    embed(u)
+            turns = waiting + [(u, b0) for u in steps for b0 in (0, 2)]
+            waiting = [turns.pop()] if kind in ("double", "single") else []
+            for u, b0 in turns:
+                turn(u, b0, b0 + 2)
+            fills = [(u, b0 + j) for u, b0 in turns for j in (0, 1)]
+            for word in order.split():
+                if word == "W":
+                    for ts in halves:
+                        group_w(*later_w[i], ts)
+                elif word == "Q":
+                    quantize_w(*later_w[i], slice(0, PACK))
+                elif word[0] in "gq":
+                    j = int(word[1])
+                    part = (s, 2 * j, 2 * j + 2) if kind == "last" else (steps[j], 0, BLOCKS)
+                    if word[0] == "g":
+                        group_y(*part)
+                    else:
+                        quantize_y(*part)
+                        g, c = divmod(part[0], CHUNKS)
+                        if kind == "last" and ONCE:
+                            if j == 1:
+                                store_codes(g, c * CHUNK, M)
+                        elif kind != "double":
+                            store_codes(g, c * CHUNK + part[1] * P, c * CHUNK + part[2] * P)
+                        elif j == 1:
+                            store_codes(g, (c - 1) * CHUNK, (c + 1) * CHUNK)
+                else:
+                    u, b = fills[int(word[1])]
+                    empty(u, b, word[0] == "S")
+                    emptied.add((u, b))
+                    if kind == "last" and b // 2 in SINGLY:
+                        store_rows(u, b, b + 1)
+                    elif (u, b ^ 1) in emptied:
+                        store_rows(u, b // 2 * 2, b // 2 * 2 + 2)
+            s += len(steps)

from contextlib import ExitStack

import concourse.mybir as mybir
from concourse.masks import make_identity

M, K, N = 2048, 1024, 1536
FLOPS = 2 * M * K * N

F32 = mybir.dt.float32
BF16 = mybir.dt.bfloat16
I32 = mybir.dt.int32
U32 = mybir.dt.uint32
U8 = mybir.dt.uint8
FP8X4 = mybir.dt.float8_e4m3fn_x4
SILU = mybir.ActivationFunctionType.Silu

P = 128
PACK = 4
SPAN = P * PACK
PASSES = K // SPAN
GROUPS = N // SPAN
CHUNK = 512
CHUNKS = M // CHUNK
BLOCKS = CHUNK // P
STEPS = GROUPS * CHUNKS
QUADS = 4
BANKS = 8
PLAN = [('double', 'W g0 Q q0 S0 S1 V2 V3 g1 S4 V5 q1'), ('double', 'W g0 Q S0 S1 S2 S3 V4 V5 g1 V6 S7 q0 q1'), ('double', 'W g0 Q S0 S1 S2 S3 V4 V5 g1 V6 S7 q0 q1'), ('single', 'S0 S1 V2 W S3 g0 Q q0'), ('single', 'S0 S1 V2 V3 g0 q0'), ('single', 'S0 S1 V2 V3 g0 q0'), ('single', 'S0 S1 V2 V3 g0 q0'), ('whole', 'V0 S1 S2 S3 g0 V4 V5 q0'), ('last', 'g0 S0 S1 g1 V2 q0 S3 q1')]
SINGLY = (0, 1)
ONCE = True


def tile_timestep_embedding_silu_g6_kernel(tc, x_words, x_scales, w, bias, out_0, out_1, out_2):
    nc = tc.nc
    with ExitStack() as ctx:
        keep = ctx.enter_context(tc.tile_pool(name="keep", bufs=1))
        flow = ctx.enter_context(tc.tile_pool(name="flow", bufs=4))
        psum = ctx.enter_context(tc.psum_pool(name="psum", bufs=1))
        ctx.enter_context(tc.manual_schedule())

        x_codes = keep.tile([P, PASSES, M], U32, name="x_codes", align_bytes=64)
        x_plane = [keep.tile([P, CHUNK], U8, name="x_plane%d" % k, align_bytes=64) for k in range(PASSES)]
        w_raw = {}
        w_codes = {}
        w_plane = {}
        for g in range(GROUPS):
            for k in range(PASSES):
                w_raw[g, k] = keep.tile([P, PACK, SPAN], BF16, name="w_raw%d%d" % (g, k), align_bytes=64)
                w_codes[g, k] = keep.tile([P, SPAN], U32, name="w_codes%d%d" % (g, k), align_bytes=64)
                w_plane[g, k] = keep.tile([P, SPAN], U8, name="w_plane%d%d" % (g, k), align_bytes=64)
        y_plane = [keep.tile([P, CHUNK], U8, name="y_plane%d" % g, align_bytes=64) for g in range(GROUPS)]
        bias_sb = keep.tile([P, GROUPS, PACK], BF16, name="bias_sb")
        ident = keep.tile([P, P], F32, name="ident")

        x_bytes = x_words.rearrange("k p m t -> p k (m t)")
        y_bytes = out_1.rearrange("g p m t -> g p (m t)")

        def load_w(g, k):
            rows = w[k * SPAN:(k + 1) * SPAN, g * SPAN:(g + 1) * SPAN]
            nc.sync.dma_start(out=w_raw[g, k][:], in_=rows.rearrange("(p j) n -> p j n", j=PACK))

        def load_x(c0, c1, passes):
            src = x_bytes[:, passes, c0 * CHUNK * PACK:c1 * CHUNK * PACK]
            nc.sync.dma_start(out=x_codes[:, passes, c0 * CHUNK:c1 * CHUNK].bitcast(I32), in_=src.bitcast(I32))

        def load_x_plane(k):
            for q in range(QUADS):
                rows = x_scales[k, 4 * q:4 * q + 4, :].rearrange("r (c m) -> c r m", c=CHUNKS)
                nc.sync.dma_start(out=x_plane[k][32 * q:32 * q + 16, :].bitcast(I32), in_=rows.bitcast(I32))

        w_grouped = {}

        def group_w(g, k, ts):
            if (g, k) not in w_grouped:
                w_grouped[g, k] = flow.tile([P, PACK, P, PACK], BF16, name="w_grouped", bufs=2, align_bytes=64)
            src = w_raw[g, k][:].rearrange("p j (m t) -> p m t j", t=PACK)
            dst = w_grouped[g, k][:].rearrange("p t m j -> p m t j")
            nc.vector.tensor_copy(out=dst[:, :, ts, :], in_=src[:, :, ts, :])

        def quantize_w(g, k, ts):
            cols = slice(ts.start * P, ts.stop * P)
            nc.vector.quantize_mx(
                out=w_codes[g, k][:, cols].bitcast(FP8X4),
                scales=w_plane[g, k][:, cols],
                in_=w_grouped[g, k][:, ts, :, :].rearrange("p t m j -> p (t m j)"),
            )

        y_codes = {}
        acc = {}
        y_t = {}
        y_grouped = {}
        turned = {}
        y_rows = {}
        fills_so_far = list(reversed(range(200)))

        def next_bank(shape):
            return psum.tile(shape, F32, name="bank", tag="bank%d" % (fills_so_far.pop() % BANKS))

        def multiply(s, t, k, b0=0, b1=BLOCKS):
            g, c = divmod(s, CHUNKS)
            if k == 0:
                acc[s, t, b0] = next_bank([P, (b1 - b0) * P])
            cols = slice(t * P, (t + 1) * P)
            nc.tensor.matmul_mx(
                out=acc[s, t, b0][:],
                lhsT=w_codes[g, k][:, cols].bitcast(FP8X4),
                lhsT_scale=w_plane[g, k][:, cols],
                rhs=x_codes[:, k, c * CHUNK + b0 * P:c * CHUNK + b1 * P].bitcast(FP8X4),
                rhs_scale=x_plane[k][4 * c:, b0 * P:b1 * P],
                start=(k == 0),
                stop=(k == PASSES - 1),
            )

        def activate(s, t, b0=0, b1=BLOCKS):
            g = s // CHUNKS
            if s not in y_t:
                y_t[s] = flow.tile([P, PACK, CHUNK], F32, name="y_t", bufs=5)
            nc.scalar.activation(
                out=y_t[s][:, t, b0 * P:b1 * P], in_=acc[s, t, b0][:], func=SILU, bias=bias_sb[:, g, t:t + 1]
            )

        def embed(s, b0=0, b1=BLOCKS):
            for t in range(PACK):
                for k in range(PASSES):
                    multiply(s, t, k, b0, b1)
                activate(s, t, b0, b1)

        def turn(s, b0, b1):
            if s not in y_rows:
                y_rows[s] = flow.tile([P, BLOCKS, SPAN], F32, name="y_rows", bufs=6)
            for b in range(b0, b1):
                turned[s, b] = next_bank([P, PACK, P])
            for t in range(PACK):
                for b in range(b0, b1):
                    nc.tensor.transpose(turned[s, b][:, t, :], y_t[s][:, t, b * P:(b + 1) * P], ident[:])

        def empty(s, b, on_scalar):
            dst = y_rows[s][:, b, :].rearrange("m (p t) -> m p t", t=PACK)
            src = turned[s, b][:].rearrange("m t p -> m p t")
            if on_scalar:
                nc.scalar.copy(out=dst, in_=src)
            else:
                nc.vector.tensor_copy(out=dst, in_=src)

        def store_rows(s, b0, b1):
            g, c = divmod(s, CHUNKS)
            rows = out_0[c * CHUNK + b0 * P:c * CHUNK + b1 * P, g * SPAN:(g + 1) * SPAN]
            nc.sync.dma_start(out=rows.rearrange("(b m) n -> m b n", m=P), in_=y_rows[s][:, b0:b1, :])

        def group_y(s, b0=0, b1=BLOCKS):
            y_grouped[s, b0] = flow.tile([P, (b1 - b0) * P, PACK], BF16, name="y_grouped", bufs=3, align_bytes=64)
            nc.vector.tensor_copy(
                out=y_grouped[s, b0][:].rearrange("p (c i) t -> p c t i", i=4),
                in_=y_t[s][:, :, b0 * P:b1 * P].rearrange("p t (c i) -> p c t i", i=4),
            )

        def quantize_y(s, b0=0, b1=BLOCKS):
            g, c = divmod(s, CHUNKS)
            if g not in y_codes:
                y_codes[g] = flow.tile([P, M], U32, name="y_codes", bufs=2, align_bytes=64)
            nc.vector.quantize_mx(
                out=y_codes[g][:, c * CHUNK + b0 * P:c * CHUNK + b1 * P].bitcast(FP8X4),
                scales=y_plane[g][4 * c:, b0 * P:b1 * P],
                in_=y_grouped[s, b0][:].rearrange("p m t -> p (m t)"),
            )

        def store_codes(g, m0, m1):
            nc.sync.dma_start(out=y_bytes[g][:, m0 * PACK:m1 * PACK].bitcast(I32), in_=y_codes[g][:, m0:m1].bitcast(I32))
            if m1 == M:
                for q in range(QUADS):
                    rows = out_2[g, 4 * q:4 * q + 4, :].rearrange("r (c m) -> c r m", c=CHUNKS)
                    nc.sync.dma_start(out=rows.bitcast(I32), in_=y_plane[g][32 * q:32 * q + 16, :].bitcast(I32))

        for k in range(PASSES):
            nc.vector.memset(x_plane[k][:].bitcast(I32), 0)
        nc.scalar.dma_start(out=bias_sb[:], in_=bias.rearrange("(g p t) -> p g t", p=P, t=PACK))
        make_identity(nc, ident[:])
        for k in range(PASSES):
            load_w(0, k)
            load_x(0, 1, slice(k, k + 1))
            load_x_plane(k)
        both = slice(0, PASSES)
        load_x(1, 2, both)
        load_w(1, 0)
        load_x(2, 4, both)
        load_w(1, 1)
        load_w(2, 0)
        load_w(2, 1)

        halves = (slice(0, 2), slice(2, 4))
        for k in range(PASSES):
            for ts in halves:
                group_w(0, k, ts)
                quantize_w(0, k, ts)
                for t in range(ts.start, ts.stop):
                    multiply(0, t, k)
                    if k == PASSES - 1:
                        activate(0, t)

        later_w = [(g, k) for g in range(1, GROUPS) for k in range(PASSES)]
        emptied = set()
        s = 0
        waiting = []
        for i, (kind, order) in enumerate(PLAN):
            steps = [s, s + 1] if kind == "double" else [s]
            for u in steps:
                if kind == "last":
                    embed(u, 0, 2)
                    embed(u, 2, 4)
                elif u > 0:
                    embed(u)
            turns = waiting + [(u, b0) for u in steps for b0 in (0, 2)]
            waiting = [turns.pop()] if kind in ("double", "single") else []
            for u, b0 in turns:
                turn(u, b0, b0 + 2)
            fills = [(u, b0 + j) for u, b0 in turns for j in (0, 1)]
            for word in order.split():
                if word == "W":
                    for ts in halves:
                        group_w(*later_w[i], ts)
                elif word == "Q":
                    quantize_w(*later_w[i], slice(0, PACK))
                elif word[0] in "gq":
                    j = int(word[1])
                    part = (s, 2 * j, 2 * j + 2) if kind == "last" else (steps[j], 0, BLOCKS)
                    if word[0] == "g":
                        group_y(*part)
                    else:
                        quantize_y(*part)
                        g, c = divmod(part[0], CHUNKS)
                        if kind == "last" and ONCE:
                            if j == 1:
                                store_codes(g, c * CHUNK, M)
                        elif kind != "double":
                            store_codes(g, c * CHUNK + part[1] * P, c * CHUNK + part[2] * P)
                        elif j == 1:
                            store_codes(g, (c - 1) * CHUNK, (c + 1) * CHUNK)
                else:
                    u, b = fills[int(word[1])]
                    empty(u, b, word[0] == "S")
                    emptied.add((u, b))
                    if kind == "last" and b // 2 in SINGLY:
                        store_rows(u, b, b + 1)
                    elif (u, b ^ 1) in emptied:
                        store_rows(u, b // 2 * 2, b // 2 * 2 + 2)
            s += len(steps)
